import numpy as np
import ml_dtypes


def mxq(x, axis, fmt="e4m3"):
    dtype, down = {"e4m3": (ml_dtypes.float8_e4m3fn, 7), "e5m2": (ml_dtypes.float8_e5m2, 14)}[fmt]
    v = np.moveaxis(np.asarray(x, np.float32).astype(ml_dtypes.bfloat16).astype(np.float64), axis, -1)
    blocks = v.reshape(v.shape[:-1] + (-1, 32))
    amax = np.abs(blocks).max(-1, keepdims=True)
    byte = np.maximum(np.where(amax > 0, np.frexp(amax)[1] - 1 + 127, 0) - down, 1)
    scale = np.exp2(byte - 127.0)
    codes = (blocks / scale).astype(np.float32).astype(dtype).astype(np.float64)
    return np.moveaxis((codes * scale).reshape(v.shape), -1, axis)


WIDE = False


def mx_kscale(k):
    if not WIDE:
        return np.ones(k)
    levels = np.array([30, -30])
    if k % 512:
        return np.exp2(np.random.permutation(np.resize(levels, k // 32))).repeat(32)
    a = np.empty((k // 512, 16))
    for p in range(k // 512):
        a[p, :8] = np.random.permutation(np.resize(levels, 8))
        for g in range(8):
            far = levels[np.abs(levels - a[p, g]) >= 10]
            a[p, g + 8] = far[np.random.randint(len(far))]
    return np.exp2(a.ravel()).repeat(32)


def f64(x):
    return np.asarray(x).astype(np.float64)


def striped(idx):
    return np.tile(np.asarray(idx).reshape(-1, 16).T, (8, 1)).astype(np.uint16)


def unstriped(offs):
    return offs[:16].T.reshape(-1).astype(np.int64)


E2M1 = np.array([0.0, 0.5, 1.0, 1.5, 2.0, 3.0, 4.0, 6.0, -0.0, -0.5, -1.0, -1.5, -2.0, -3.0, -4.0, -6.0])


def pack_weight(w, fmt):
    k, n = w.shape
    w = f64(np.asarray(w, np.float32).astype(ml_dtypes.bfloat16)).reshape(k // 32, 32, n)
    amax = np.abs(w).max(1)
    if fmt in ("e4m3", "e5m2"):
        byte = np.frexp(amax)[1] - 1 + 127 - (7 if fmt == "e4m3" else 14)
    else:
        mant, ex = np.frexp(amax / 6.0)
        byte = np.where(mant > 0.5, ex, ex - 1) + 127
    byte = np.clip(np.where(amax > 0, byte, 1), 1, 254)
    scaled = (w * np.exp2(127.0 - byte)[:, None, :]).reshape(k, n).astype(np.float32)
    by_word = np.ascontiguousarray(scaled.reshape(k // 512, 128, 4, n).transpose(0, 1, 3, 2))
    if fmt in ("e4m3", "e5m2"):
        words = by_word.astype(ml_dtypes.float8_e4m3fn if fmt == "e4m3" else ml_dtypes.float8_e5m2).view(np.uint8)
    else:
        c = by_word.astype(ml_dtypes.float4_e2m1fn).view(np.uint8) & 0xF
        words = (c[..., 0::2] | (c[..., 1::2] << 4)).reshape(k // 512, 128, 2 * n)
    return np.ascontiguousarray(words), np.ascontiguousarray(byte.astype(np.uint8).reshape(k // 512, 16, n))


def unpack_weight(words, scales, fmt):
    g, _, n = scales.shape
    words = np.ascontiguousarray(words).reshape(g, 128, n, -1)
    if fmt in ("e4m3", "e5m2"):
        vals = words.view(ml_dtypes.float8_e4m3fn if fmt == "e4m3" else ml_dtypes.float8_e5m2).astype(np.float64)
    else:
        nib = np.empty((g, 128, n, 4), np.uint8)
        nib[..., 0::2] = words & 0xF
        nib[..., 1::2] = words >> 4
        vals = E2M1[nib]
    vals = vals * np.repeat(np.exp2(scales.astype(np.float64) - 127.0), 8, axis=1)[..., None]
    return vals.transpose(0, 1, 3, 2).reshape(g * 512, n)


K, T, J, I, R, V, G = 512, 512, 256, 256, 512, 512, 32


def setup_inputs():
    n = np.random.standard_normal
    idx = np.random.permutation(T)[:J]
    idx2 = np.random.permutation(V)[:J]
    idx3 = np.random.permutation(T)[:I]
    fk = mx_kscale(K)
    fr = mx_kscale(R)
    xtp = pack_weight(n((K, T)) / fk[:, None], "e2m1")
    wap = pack_weight(n((K, R)) * 0.5 / np.sqrt(K) * fk[:, None] * fr, "e5m2")
    wbp = pack_weight(n((K, R)) * 1 / np.sqrt(K) * fk[:, None] / fr, "e4m3")
    return {
        "xt_words": xtp[0],
        "xt_scales": xtp[1],
        "wa_words": wap[0],
        "wa_scales": wap[1],
        "tb": (n((R, V)) * 0.5 * fr[:, None]).astype(np.float32),
        "wb_words": wbp[0],
        "wb_scales": wbp[1],
        "tg": (np.random.uniform(-10.0, 20.0, (J, 1))).astype(np.float32),
        "cw1": (np.random.uniform(0.5, 2.0, (1, I))).astype(np.float32),
        "offs": striped(idx),
        "offs2": striped(idx2),
        "offs3": striped(idx3),
    }


def reference(xt_words, xt_scales, wa_words, wa_scales, tb, wb_words, wb_scales, tg, cw1, offs, offs2, offs3):
    idx = unstriped(offs)
    idx2 = unstriped(offs2)
    idx3 = unstriped(offs3)
    xtu = unpack_weight(xt_words, xt_scales, "e2m1")
    wau = unpack_weight(wa_words, wa_scales, "e5m2")
    wbu = unpack_weight(wb_words, wb_scales, "e4m3")
    xtidxg = xtu[:, idx]
    za = wau.T @ xtidxg
    ha = np.maximum(za - f64(tb)[:, idx2], 0.0)
    xtidx3g = xtu[:, idx3]
    zb = wbu.T @ xtidx3g
    mb1 = zb.reshape(R, G, I // G).mean(axis=2)
    mb2 = np.repeat(mb1, I // G, axis=1)
    hb = zb - mb2
    haq = mxq(ha, 0, "e5m2")
    hbq = mxq(hb, 0, "e5m2")
    a0 = haq.T @ hbq
    y = 0.04 * np.maximum(a0 - f64(tg), 0.0) * f64(cw1)
    return y

@@ -1,0 +1,187 @@
+from contextlib import ExitStack
+
+import concourse.mybir as mybir
+
+K, T, J, I, R, V, G = 512, 512, 256, 256, 512, 512, 32
+FLOPS = 2 * K * R * J + 2 * K * R * I + 2 * R * J * I
+
+F32 = mybir.dt.float32
+BF16 = mybir.dt.bfloat16
+I32 = mybir.dt.int32
+U32 = mybir.dt.uint32
+U16 = mybir.dt.uint16
+U8 = mybir.dt.uint8
+E2M1 = mybir.dt.float4_e2m1fn_x4
+E4M3 = mybir.dt.float8_e4m3fn_x4
+E5M2 = mybir.dt.float8_e5m2_x4
+ALU = mybir.AluOpType
+ACT = mybir.ActivationFunctionType
+
+P = 128
+PACK = 4
+HALF = 128
+BUNDLE = I // G
+RUN = 8
+
+
+def tile_list_meet_overtable_levelled_hinge_kernel(
+    tc, xt_words, xt_scales, wa_words, wa_scales, tb, wb_words, wb_scales, tg, cw1, offs, offs2, offs3, out
+):
+    nc = tc.nc
+    with ExitStack() as ctx:
+        sb = ctx.enter_context(tc.tile_pool(name="sb", bufs=1))
+        ps = ctx.enter_context(tc.psum_pool(name="ps", bufs=1))
+
+        def load_scales(queue, plane, scales):
+            rows = scales[0].bitcast(I32)
+            for q in range(4):
+                queue.dma_start(
+                    out=plane[:].bitcast(I32)[32 * q : 32 * q + 32, :],
+                    in_=rows[4 * q : 4 * q + 4, :].unsqueeze(0).broadcast_to([8, 4, R // 4]),
+                )
+
+        list_a = sb.tile([P, J // 16], U16, name="list_a")
+        list_t = sb.tile([P, J // 16], U16, name="list_t")
+        list_b = sb.tile([P, I // 16], U16, name="list_b")
+        x_words = sb.tile([P, T], U16, name="x_words", align_bytes=64)
+        x_plane = sb.tile([P, T], U8, name="x_plane", align_bytes=64)
+        wa_raw = sb.tile([P, R], I32, name="wa_raw", align_bytes=64)
+        wb_raw = sb.tile([P, R], I32, name="wb_raw", align_bytes=64)
+        wa_plane_raw = sb.tile([P, R], U8, name="wa_plane_raw", align_bytes=64)
+        wb_plane_raw = sb.tile([P, R], U8, name="wb_plane_raw", align_bytes=64)
+        table = [sb.tile([P, V], F32, name="table%d" % t, align_bytes=64) for t in range(PACK)]
+        target = sb.tile([P, 2], F32, name="target")
+        weight = sb.tile([P, I], F32, name="weight")
+
+        nc.sync.dma_start(list_b[:], offs3)
+        nc.sync.dma_start(out=x_words[:].bitcast(I32), in_=xt_words[0].bitcast(I32))
+        load_scales(nc.scalar, x_plane, xt_scales)
+        nc.sync.dma_start(out=wb_raw[:], in_=wb_words[0].rearrange("p n t -> p (n t)").bitcast(I32))
+        tb_runs = tb.rearrange("(b t q) v -> t b q v", t=PACK, q=RUN)
+        nc.sync.dma_start(out=table[0][:], in_=tb_runs[0])
+        load_scales(nc.gpsimd, wa_plane_raw, wa_scales)
+        load_scales(nc.sync, wb_plane_raw, wb_scales)
+        nc.sync.dma_start(list_a[:], offs)
+        nc.sync.dma_start(list_t[:], offs2)
+        nc.sync.dma_start(out=wa_raw[:], in_=wa_words[0].rearrange("p n t -> p (n t)").bitcast(I32))
+        for t in range(1, PACK):
+            nc.sync.dma_start(out=table[t][:], in_=tb_runs[t])
+        with nc.allow_non_contiguous_dma(reason="one target a partition"):
+            nc.sync.dma_start(out=target[:], in_=tg.rearrange("(h p) o -> p (h o)", p=P))
+        nc.sync.dma_start(out=weight[:], in_=cw1[0].partition_broadcast(P))
+
+        def pick_tokens(name, offsets):
+            words = sb.tile([P, J], U16, name=name + "_words", align_bytes=64)
+            plane = sb.tile([P, J], U8, name=name + "_plane", align_bytes=64)
+            nc.vector.tensor_copy(words[:], x_words[:].indirect(offsets[:]))
+            nc.vector.tensor_copy(plane[:], x_plane[:].indirect(offsets[:]))
+            return words, plane
+
+        def deal(name, raw, plane_raw, plane_engine):
+            words = sb.tile([P, R], I32, name=name + "_dealt", align_bytes=64)
+            plane = sb.tile([P, R], U8, name=name + "_plane_dealt", align_bytes=64)
+            nc.scalar.copy(
+                out=words[:].bitcast(U32).rearrange("p (t b q) -> p t b q", t=PACK, q=RUN),
+                in_=raw[:].bitcast(U32).rearrange("p (b t q) -> p t b q", t=PACK, q=RUN),
+            )
+            plane_engine.tensor_copy(
+                out=plane[:].bitcast(I32).rearrange("p (t b q) -> p t b q", t=PACK, q=RUN // 4),
+                in_=plane_raw[:].bitcast(I32).rearrange("p (b t q) -> p t b q", t=PACK, q=RUN // 4),
+            )
+            return words, plane
+
+        def first_stage(target_cols, t, w, w_dtype, x, cols):
+            feats = slice(t * P, (t + 1) * P)
+            nc.tensor.matmul_mx(
+                out=target_cols,
+                lhsT=w[0][:, feats].bitcast(w_dtype),
+                lhsT_scale=w[1][:, feats],
+                rhs=x[0][:, cols].bitcast(E2M1),
+                rhs_scale=x[1][:, cols],
+                start=True,
+                stop=True,
+            )
+
+        xb = pick_tokens("xb", list_b)
+        wb = deal("wb", wb_raw, wb_plane_raw, nc.vector)
+        xa = pick_tokens("xa", list_a)
+        zb = [ps.tile([P, PACK, HALF], F32, name="zb%d" % h) for h in range(2)]
+        for h in range(2):
+            for t in range(PACK):
+                first_stage(zb[h][:, t, :], t, wb, E4M3, xb, slice(h * HALF, (h + 1) * HALF))
+        wa = deal("wa", wa_raw, wa_plane_raw, nc.gpsimd)
+        za = [ps.tile([P, 2, J], F32, name="za%d" % u) for u in range(2)]
+        for t in range(PACK):
+            first_stage(za[t // 2][:, t % 2, :], t, wa, E5M2, xa, slice(0, J))
+
+        picked = sb.tile([P, PACK, J], F32, name="picked")
+        for t in range(PACK):
+            nc.scalar.activation(picked[:, t, :], table[t][:].indirect(list_t[:]), ACT.Copy)
+        minus_target = sb.tile([P, 2], F32, name="minus_target")
+        nc.gpsimd.tensor_scalar(minus_target[:], target[:], -1.0, 0.0, ALU.mult, ALU.add)
+
+        nb = HALF // BUNDLE
+        sums = sb.tile([P, 2, nb, PACK], F32, name="sums")
+        means = sb.tile([P, 2, nb, PACK], F32, name="means")
+        for h in range(2):
+            nc.vector.tensor_reduce(
+                out=sums[:, h],
+                in_=zb[h][:].rearrange("p t (g e) -> p g t e", e=BUNDLE),
+                axis=mybir.AxisListType.X,
+                op=ALU.add,
+            )
+            nc.gpsimd.tensor_scalar(
+                means[:, h].rearrange("p g t -> p (g t)"),
+                sums[:, h].rearrange("p g t -> p (g t)"),
+                1.0 / BUNDLE,
+                0.0,
+                ALU.mult,
+                ALU.add,
+            )
+
+        def quantise(name, values, width):
+            words = sb.tile([P, width], U32, name=name + "_q", align_bytes=64)
+            plane = sb.tile([P, width], U8, name=name + "_s", align_bytes=64)
+            nc.vector.quantize_mx(
+                out=words[:].bitcast(E5M2), scales=plane[:], in_=values[:].rearrange("p c t -> p (c t)")
+            )
+            return words, plane
+
+        hb = sb.tile([P, I, PACK], BF16, name="hb", align_bytes=64)
+        for h in range(2):
+            nc.vector.tensor_tensor(
+                hb[:, h * HALF : (h + 1) * HALF, :].rearrange("p (g e) t -> p g e t", e=BUNDLE),
+                zb[h][:].rearrange("p t (g e) -> p g e t", e=BUNDLE),
+                means[:, h].unsqueeze(2).broadcast_to([P, nb, BUNDLE, PACK]),
+                ALU.subtract,
+            )
+        diff = sb.tile([P, PACK, J], F32, name="diff")
+        for t in range(PACK):
+            nc.vector.tensor_tensor(diff[:, t, :], za[t // 2][:, t % 2, :], picked[:, t, :], ALU.subtract)
+        hbq = quantise("hb", hb, I)
+
+        ha = [sb.tile([P, HALF, PACK], BF16, name="ha%d" % h, align_bytes=64) for h in range(2)]
+        lines_out = [ha[h][:].rearrange("p (c n) t -> p c t n", n=4) for h in range(2)]
+        lines_in = [diff[:, :, h * HALF : (h + 1) * HALF].rearrange("p t (c n) -> p c t n", n=4) for h in range(2)]
+        nc.scalar.activation(lines_out[1], lines_in[1], ACT.Relu)
+        nc.vector.tensor_scalar(lines_out[0], lines_in[0], 0.0, None, ALU.max)
+
+        for h in range(2):
+            haq = quantise("ha%d" % h, ha[h], HALF)
+            for c in range(2):
+                cols = slice(c * HALF, (c + 1) * HALF)
+                score = ps.tile([P, HALF], F32, name="score%d%d" % (h, c))
+                nc.tensor.matmul_mx(
+                    out=score[:],
+                    lhsT=haq[0][:].bitcast(E5M2),
+                    lhsT_scale=haq[1][:],
+                    rhs=hbq[0][:, cols].bitcast(E5M2),
+                    rhs_scale=hbq[1][:, cols],
+                    start=True,
+                    stop=True,
+                )
+                excess = sb.tile([P, HALF], F32, name="excess%d%d" % (h, c))
+                nc.scalar.activation(excess[:], score[:], ACT.Relu, bias=minus_target[:, h : h + 1])
+                result = sb.tile([P, HALF], F32, name="result%d%d" % (h, c))
+                nc.vector.scalar_tensor_tensor(result[:], excess[:], 0.04, weight[:, cols], ALU.mult, ALU.mult)
+                nc.sync.dma_start(out=out[h * P : (h + 1) * P, cols], in_=result[:])

@@ -1,6 +1,7 @@
 from contextlib import ExitStack
 
 import concourse.mybir as mybir
+from concourse.masks import make_identity
 
 K, T, J, I, R, V, G = 512, 512, 256, 256, 512, 512, 32
 FLOPS = 2 * K * R * J + 2 * K * R * I + 2 * R * J * I
@@ -32,12 +33,12 @@ def tile_list_meet_overtable_levelled_hinge_kernel(
         sb = ctx.enter_context(tc.tile_pool(name="sb", bufs=1))
         ps = ctx.enter_context(tc.psum_pool(name="ps", bufs=1))
 
-        def load_scales(queue, plane, scales):
+        def load_scales(queue, plane, scales, copies):
             rows = scales[0].bitcast(I32)
             for q in range(4):
                 queue.dma_start(
-                    out=plane[:].bitcast(I32)[32 * q : 32 * q + 32, :],
-                    in_=rows[4 * q : 4 * q + 4, :].unsqueeze(0).broadcast_to([8, 4, R // 4]),
+                    out=plane[:].bitcast(I32)[32 * q : 32 * q + 4 * copies, :],
+                    in_=rows[4 * q : 4 * q + 4, :].unsqueeze(0).broadcast_to([copies, 4, R // 4]),
                 )
 
         list_a = sb.tile([P, J // 16], U16, name="list_a")
@@ -51,24 +52,29 @@ def tile_list_meet_overtable_levelled_hinge_kernel(
         wb_plane_raw = sb.tile([P, R], U8, name="wb_plane_raw", align_bytes=64)
         table = [sb.tile([P, V], F32, name="table%d" % t, align_bytes=64) for t in range(PACK)]
         target = sb.tile([P, 2], F32, name="target")
-        weight = sb.tile([P, I], F32, name="weight")
+        weight_pairs = sb.tile([P, 2], F32, name="weight_pairs")
+        identity = sb.tile([P, P], F32, name="identity")
 
-        nc.sync.dma_start(list_b[:], offs3)
-        nc.sync.dma_start(out=x_words[:].bitcast(I32), in_=xt_words[0].bitcast(I32))
-        load_scales(nc.scalar, x_plane, xt_scales)
-        nc.sync.dma_start(out=wb_raw[:], in_=wb_words[0].rearrange("p n t -> p (n t)").bitcast(I32))
+        nc.vector.memset(wb_plane_raw[:].bitcast(I32), 0)
+        nc.vector.memset(wa_plane_raw[:].bitcast(I32), 0)
         tb_runs = tb.rearrange("(b t q) v -> t b q v", t=PACK, q=RUN)
-        nc.sync.dma_start(out=table[0][:], in_=tb_runs[0])
-        load_scales(nc.gpsimd, wa_plane_raw, wa_scales)
-        load_scales(nc.sync, wb_plane_raw, wb_scales)
+        for t in range(2):
+            nc.gpsimd.dma_start(out=table[t][:], in_=tb_runs[t])
+        make_identity(nc, identity[:])
+        nc.sync.dma_start(list_b[:], offs3)
+        load_scales(nc.scalar, x_plane, xt_scales, 8)
         nc.sync.dma_start(list_a[:], offs)
+        nc.sync.dma_start(out=x_words[:].bitcast(I32), in_=xt_words[0].bitcast(I32))
+        nc.sync.dma_start(out=wb_raw[:], in_=wb_words[0].rearrange("p n t -> p (n t)").bitcast(I32))
+        load_scales(nc.sync, wb_plane_raw, wb_scales, 1)
         nc.sync.dma_start(list_t[:], offs2)
         nc.sync.dma_start(out=wa_raw[:], in_=wa_words[0].rearrange("p n t -> p (n t)").bitcast(I32))
-        for t in range(1, PACK):
-            nc.sync.dma_start(out=table[t][:], in_=tb_runs[t])
+        nc.sync.dma_start(out=table[2][:], in_=tb_runs[2])
+        load_scales(nc.sync, wa_plane_raw, wa_scales, 1)
+        nc.sync.dma_start(out=table[3][:], in_=tb_runs[3])
         with nc.allow_non_contiguous_dma(reason="one target a partition"):
             nc.sync.dma_start(out=target[:], in_=tg.rearrange("(h p) o -> p (h o)", p=P))
-        nc.sync.dma_start(out=weight[:], in_=cw1[0].partition_broadcast(P))
+        nc.sync.dma_start(out=weight_pairs[:], in_=cw1.rearrange("o (p e) -> p (o e)", e=2))
 
         def pick_tokens(name, offsets):
             words = sb.tile([P, J], U16, name=name + "_words", align_bytes=64)
@@ -77,16 +83,16 @@ def tile_list_meet_overtable_levelled_hinge_kernel(
             nc.vector.tensor_copy(plane[:], x_plane[:].indirect(offsets[:]))
             return words, plane
 
-        def deal(name, raw, plane_raw, plane_engine):
+        def deal(name, raw, plane_raw, word_copy, view):
             words = sb.tile([P, R], I32, name=name + "_dealt", align_bytes=64)
             plane = sb.tile([P, R], U8, name=name + "_plane_dealt", align_bytes=64)
-            nc.scalar.copy(
-                out=words[:].bitcast(U32).rearrange("p (t b q) -> p t b q", t=PACK, q=RUN),
-                in_=raw[:].bitcast(U32).rearrange("p (b t q) -> p t b q", t=PACK, q=RUN),
+            word_copy(
+                out=words[:].bitcast(view).rearrange("p (t b q) -> p t b q", t=PACK, q=RUN),
+                in_=raw[:].bitcast(view).rearrange("p (b t q) -> p t b q", t=PACK, q=RUN),
             )
-            plane_engine.tensor_copy(
-                out=plane[:].bitcast(I32).rearrange("p (t b q) -> p t b q", t=PACK, q=RUN // 4),
-                in_=plane_raw[:].bitcast(I32).rearrange("p (b t q) -> p t b q", t=PACK, q=RUN // 4),
+            nc.scalar.copy(
+                out=plane[:].bitcast(U32).rearrange("p (t b q) -> p t b q", t=PACK, q=RUN // 4),
+                in_=plane_raw[:].bitcast(U32).rearrange("p (b t q) -> p t b q", t=PACK, q=RUN // 4),
             )
             return words, plane
 
@@ -103,85 +109,103 @@ def tile_list_meet_overtable_levelled_hinge_kernel(
             )
 
         xb = pick_tokens("xb", list_b)
-        wb = deal("wb", wb_raw, wb_plane_raw, nc.vector)
+        wb = deal("wb", wb_raw, wb_plane_raw, nc.scalar.copy, U32)
         xa = pick_tokens("xa", list_a)
-        zb = [ps.tile([P, PACK, HALF], F32, name="zb%d" % h) for h in range(2)]
+        zb = [ps.tile([P, PACK, HALF], F32, name="zb%d" % h, tag="bank%d" % h) for h in range(2)]
         for h in range(2):
             for t in range(PACK):
                 first_stage(zb[h][:, t, :], t, wb, E4M3, xb, slice(h * HALF, (h + 1) * HALF))
-        wa = deal("wa", wa_raw, wa_plane_raw, nc.gpsimd)
-        za = [ps.tile([P, 2, J], F32, name="za%d" % u) for u in range(2)]
-        for t in range(PACK):
-            first_stage(za[t // 2][:, t % 2, :], t, wa, E5M2, xa, slice(0, J))
+        wa = deal("wa", wa_raw, wa_plane_raw, nc.vector.tensor_copy, I32)
+        za = [ps.tile([P, PACK, HALF], F32, name="za%d" % h) for h in range(2)]
+        for h in range(2):
+            for t in range(PACK):
+                first_stage(za[h][:, t, :], t, wa, E5M2, xa, slice(h * HALF, (h + 1) * HALF))
 
-        picked = sb.tile([P, PACK, J], F32, name="picked")
+        picked = sb.tile([P, PACK, J], F32, name="picked", tag="picked", align_bytes=64)
         for t in range(PACK):
             nc.scalar.activation(picked[:, t, :], table[t][:].indirect(list_t[:]), ACT.Copy)
-        minus_target = sb.tile([P, 2], F32, name="minus_target")
-        nc.gpsimd.tensor_scalar(minus_target[:], target[:], -1.0, 0.0, ALU.mult, ALU.add)
 
         nb = HALF // BUNDLE
-        sums = sb.tile([P, 2, nb, PACK], F32, name="sums")
-        means = sb.tile([P, 2, nb, PACK], F32, name="means")
-        for h in range(2):
+        sums = sb.tile([P, 2, nb, PACK], F32, name="sums", tag="sums")
+        means = [sb.tile([P, nb, PACK], F32, name="means%d" % c, tag="means%d" % c) for c in range(2)]
+        for c in range(2):
             nc.vector.tensor_reduce(
-                out=sums[:, h],
-                in_=zb[h][:].rearrange("p t (g e) -> p g t e", e=BUNDLE),
+                out=sums[:, c],
+                in_=zb[c][:].rearrange("p t (g e) -> p g t e", e=BUNDLE),
                 axis=mybir.AxisListType.X,
                 op=ALU.add,
             )
             nc.gpsimd.tensor_scalar(
-                means[:, h].rearrange("p g t -> p (g t)"),
-                sums[:, h].rearrange("p g t -> p (g t)"),
+                means[c][:].rearrange("p g t -> p (g t)"),
+                sums[:, c].rearrange("p g t -> p (g t)"),
                 1.0 / BUNDLE,
                 0.0,
                 ALU.mult,
                 ALU.add,
             )
 
-        def quantise(name, values, width):
-            words = sb.tile([P, width], U32, name=name + "_q", align_bytes=64)
-            plane = sb.tile([P, width], U8, name=name + "_s", align_bytes=64)
+        def level(c, tag):
+            hb = sb.tile([P, HALF, PACK], BF16, name="hb%d" % c, tag=tag, align_bytes=64)
+            nc.vector.tensor_tensor(
+                hb[:].rearrange("p (g e) t -> p g e t", e=BUNDLE),
+                zb[c][:].rearrange("p t (g e) -> p g e t", e=BUNDLE),
+                means[c][:].unsqueeze(2).broadcast_to([P, nb, BUNDLE, PACK]),
+                ALU.subtract,
+            )
+            return hb
+
+        def quantise(name, values):
+            words = sb.tile([P, HALF], U32, name=name + "_q", align_bytes=64)
+            plane = sb.tile([P, HALF], U8, name=name + "_s", align_bytes=64)
             nc.vector.quantize_mx(
                 out=words[:].bitcast(E5M2), scales=plane[:], in_=values[:].rearrange("p c t -> p (c t)")
             )
             return words, plane
 
-        hb = sb.tile([P, I, PACK], BF16, name="hb", align_bytes=64)
-        for h in range(2):
-            nc.vector.tensor_tensor(
-                hb[:, h * HALF : (h + 1) * HALF, :].rearrange("p (g e) t -> p g e t", e=BUNDLE),
-                zb[h][:].rearrange("p t (g e) -> p g e t", e=BUNDLE),
-                means[:, h].unsqueeze(2).broadcast_to([P, nb, BUNDLE, PACK]),
-                ALU.subtract,
-            )
-        diff = sb.tile([P, PACK, J], F32, name="diff")
-        for t in range(PACK):
-            nc.vector.tensor_tensor(diff[:, t, :], za[t // 2][:, t % 2, :], picked[:, t, :], ALU.subtract)
-        hbq = quantise("hb", hb, I)
-
+        hb = [level(0, "hb0")]
+        minus_target = sb.tile([P, 2], F32, name="minus_target", tag="means0")
+        nc.gpsimd.tensor_scalar(minus_target[:], target[:], -1.0, 0.0, ALU.mult, ALU.add)
+        weight = ps.tile([P, 2, P], F32, name="weight", tag="bank0")
+        for e in range(2):
+            nc.tensor.transpose(weight[:, e, :], weight_pairs[:, e : e + 1].to_broadcast([P, P]), identity[:])
+        weight_cols = weight[:].rearrange("p e n -> p n e")
+        diff = sb.tile([P, 2, PACK, HALF], F32, name="diff", tag="sums")
         ha = [sb.tile([P, HALF, PACK], BF16, name="ha%d" % h, align_bytes=64) for h in range(2)]
-        lines_out = [ha[h][:].rearrange("p (c n) t -> p c t n", n=4) for h in range(2)]
-        lines_in = [diff[:, :, h * HALF : (h + 1) * HALF].rearrange("p t (c n) -> p c t n", n=4) for h in range(2)]
-        nc.scalar.activation(lines_out[1], lines_in[1], ACT.Relu)
-        nc.vector.tensor_scalar(lines_out[0], lines_in[0], 0.0, None, ALU.max)
-
         for h in range(2):
-            haq = quantise("ha%d" % h, ha[h], HALF)
-            for c in range(2):
-                cols = slice(c * HALF, (c + 1) * HALF)
+            nc.vector.tensor_tensor(diff[:, h], za[h][:], picked[:, :, h * HALF : (h + 1) * HALF], ALU.subtract)
+            nc.scalar.activation(
+                ha[h][:].rearrange("p (c n) t -> p c t n", n=4),
+                diff[:, h].rearrange("p t (c n) -> p c t n", n=4),
+                ACT.Relu,
+            )
+        hb.append(level(1, "picked"))
+        hbq = [quantise("hb0", hb[0])]
+        haq = [quantise("ha%d" % h, ha[h]) for h in range(2)]
+        hbq.append(quantise("hb1", hb[1]))
+
+        for c in range(2):
+            cols = slice(c * HALF, (c + 1) * HALF)
+            for h in range(2):
                 score = ps.tile([P, HALF], F32, name="score%d%d" % (h, c))
                 nc.tensor.matmul_mx(
                     out=score[:],
-                    lhsT=haq[0][:].bitcast(E5M2),
-                    lhsT_scale=haq[1][:],
-                    rhs=hbq[0][:, cols].bitcast(E5M2),
-                    rhs_scale=hbq[1][:, cols],
+                    lhsT=haq[h][0][:].bitcast(E5M2),
+                    lhsT_scale=haq[h][1][:],
+                    rhs=hbq[c][0][:].bitcast(E5M2),
+                    rhs_scale=hbq[c][1][:],
                     start=True,
                     stop=True,
                 )
                 excess = sb.tile([P, HALF], F32, name="excess%d%d" % (h, c))
                 nc.scalar.activation(excess[:], score[:], ACT.Relu, bias=minus_target[:, h : h + 1])
                 result = sb.tile([P, HALF], F32, name="result%d%d" % (h, c))
-                nc.vector.scalar_tensor_tensor(result[:], excess[:], 0.04, weight[:, cols], ALU.mult, ALU.mult)
-                nc.sync.dma_start(out=out[h * P : (h + 1) * P, cols], in_=result[:])
+                nc.vector.scalar_tensor_tensor(
+                    result[:].rearrange("p (n e) -> p n e", e=2),
+                    excess[:].rearrange("p (n e) -> p n e", e=2),
+                    0.04,
+                    weight_cols[:, c * HALF // 2 : (c + 1) * HALF // 2, :],
+                    ALU.mult,
+                    ALU.mult,
+                )
+                queue = nc.scalar if (c, h) == (1, 1) else nc.sync
+                queue.dma_start(out=out[h * P : (h + 1) * P, cols], in_=result[:])

@@ -74,7 +74,7 @@ def tile_list_meet_overtable_levelled_hinge_kernel(
         nc.sync.dma_start(out=table[3][:], in_=tb_runs[3])
         with nc.allow_non_contiguous_dma(reason="one target a partition"):
             nc.sync.dma_start(out=target[:], in_=tg.rearrange("(h p) o -> p (h o)", p=P))
-        nc.sync.dma_start(out=weight_pairs[:], in_=cw1.rearrange("o (p e) -> p (o e)", e=2))
+            nc.sync.dma_start(out=weight_pairs[:], in_=cw1.rearrange("o (c p) -> p (o c)", p=P))
 
         def pick_tokens(name, offsets):
             words = sb.tile([P, J], U16, name=name + "_words", align_bytes=64)
@@ -168,7 +168,6 @@ def tile_list_meet_overtable_levelled_hinge_kernel(
         weight = ps.tile([P, 2, P], F32, name="weight", tag="bank0")
         for e in range(2):
             nc.tensor.transpose(weight[:, e, :], weight_pairs[:, e : e + 1].to_broadcast([P, P]), identity[:])
-        weight_cols = weight[:].rearrange("p e n -> p n e")
         diff = sb.tile([P, 2, PACK, HALF], F32, name="diff", tag="sums")
         ha = [sb.tile([P, HALF, PACK], BF16, name="ha%d" % h, align_bytes=64) for h in range(2)]
         for h in range(2):
@@ -180,12 +179,13 @@ def tile_list_meet_overtable_levelled_hinge_kernel(
             )
         hb.append(level(1, "picked"))
         hbq = [quantise("hb0", hb[0])]
-        haq = [quantise("ha%d" % h, ha[h]) for h in range(2)]
+        haq = [quantise("ha0", ha[0])]
         hbq.append(quantise("hb1", hb[1]))
+        haq.append(quantise("ha1", ha[1]))
 
-        for c in range(2):
-            cols = slice(c * HALF, (c + 1) * HALF)
-            for h in range(2):
+        for h in range(2):
+            excess = sb.tile([P, I], F32, name="excess%d" % h)
+            for c in range(2):
                 score = ps.tile([P, HALF], F32, name="score%d%d" % (h, c))
                 nc.tensor.matmul_mx(
                     out=score[:],
@@ -196,16 +196,11 @@ def tile_list_meet_overtable_levelled_hinge_kernel(
                     start=True,
                     stop=True,
                 )
-                excess = sb.tile([P, HALF], F32, name="excess%d%d" % (h, c))
-                nc.scalar.activation(excess[:], score[:], ACT.Relu, bias=minus_target[:, h : h + 1])
-                result = sb.tile([P, HALF], F32, name="result%d%d" % (h, c))
-                nc.vector.scalar_tensor_tensor(
-                    result[:].rearrange("p (n e) -> p n e", e=2),
-                    excess[:].rearrange("p (n e) -> p n e", e=2),
-                    0.04,
-                    weight_cols[:, c * HALF // 2 : (c + 1) * HALF // 2, :],
-                    ALU.mult,
-                    ALU.mult,
+                nc.scalar.activation(
+                    excess[:, c * HALF : (c + 1) * HALF], score[:], ACT.Relu, bias=minus_target[:, h : h + 1]
                 )
-                queue = nc.scalar if (c, h) == (1, 1) else nc.sync
-                queue.dma_start(out=out[h * P : (h + 1) * P, cols], in_=result[:])
+            result = sb.tile([P, I], F32, name="result%d" % h)
+            nc.vector.scalar_tensor_tensor(
+                result[:], excess[:], 0.04, weight[:].rearrange("p c n -> p (c n)"), ALU.mult, ALU.mult
+            )
+            nc.sync.dma_start(out=out[h * P : (h + 1) * P, :], in_=result[:])

from contextlib import ExitStack

import concourse.mybir as mybir
from concourse.masks import make_identity

K, T, J, I, R, V, G = 512, 512, 256, 256, 512, 512, 32
FLOPS = 2 * K * R * J + 2 * K * R * I + 2 * R * J * I

F32 = mybir.dt.float32
BF16 = mybir.dt.bfloat16
I32 = mybir.dt.int32
U32 = mybir.dt.uint32
U16 = mybir.dt.uint16
U8 = mybir.dt.uint8
E2M1 = mybir.dt.float4_e2m1fn_x4
E4M3 = mybir.dt.float8_e4m3fn_x4
E5M2 = mybir.dt.float8_e5m2_x4
ALU = mybir.AluOpType
ACT = mybir.ActivationFunctionType

P = 128
PACK = 4
HALF = 128
BUNDLE = I // G
RUN = 8


def tile_list_meet_overtable_levelled_hinge_kernel(
    tc, xt_words, xt_scales, wa_words, wa_scales, tb, wb_words, wb_scales, tg, cw1, offs, offs2, offs3, out
):
    nc = tc.nc
    with ExitStack() as ctx:
        sb = ctx.enter_context(tc.tile_pool(name="sb", bufs=1))
        ps = ctx.enter_context(tc.psum_pool(name="ps", bufs=1))

        def load_scales(queue, plane, scales, copies):
            rows = scales[0].bitcast(I32)
            for q in range(4):
                queue.dma_start(
                    out=plane[:].bitcast(I32)[32 * q : 32 * q + 4 * copies, :],
                    in_=rows[4 * q : 4 * q + 4, :].unsqueeze(0).broadcast_to([copies, 4, R // 4]),
                )

        list_a = sb.tile([P, J // 16], U16, name="list_a")
        list_t = sb.tile([P, J // 16], U16, name="list_t")
        list_b = sb.tile([P, I // 16], U16, name="list_b")
        x_words = sb.tile([P, T], U16, name="x_words", align_bytes=64)
        x_plane = sb.tile([P, T], U8, name="x_plane", align_bytes=64)
        wa_raw = sb.tile([P, R], I32, name="wa_raw", align_bytes=64)
        wb_raw = sb.tile([P, R], I32, name="wb_raw", align_bytes=64)
        wa_plane_raw = sb.tile([P, R], U8, name="wa_plane_raw", align_bytes=64)
        wb_plane_raw = sb.tile([P, R], U8, name="wb_plane_raw", align_bytes=64)
        table = [sb.tile([P, V], F32, name="table%d" % t, align_bytes=64) for t in range(PACK)]
        target = sb.tile([P, 2], F32, name="target")
        weight_pairs = sb.tile([P, 2], F32, name="weight_pairs")
        identity = sb.tile([P, P], F32, name="identity")

        nc.vector.memset(wb_plane_raw[:].bitcast(I32), 0)
        nc.vector.memset(wa_plane_raw[:].bitcast(I32), 0)
        tb_runs = tb.rearrange("(b t q) v -> t b q v", t=PACK, q=RUN)
        for t in range(2):
            nc.gpsimd.dma_start(out=table[t][:], in_=tb_runs[t])
        make_identity(nc, identity[:])
        nc.sync.dma_start(list_b[:], offs3)
        load_scales(nc.scalar, x_plane, xt_scales, 8)
        nc.sync.dma_start(list_a[:], offs)
        nc.sync.dma_start(out=x_words[:].bitcast(I32), in_=xt_words[0].bitcast(I32))
        nc.sync.dma_start(out=wb_raw[:], in_=wb_words[0].rearrange("p n t -> p (n t)").bitcast(I32))
        load_scales(nc.sync, wb_plane_raw, wb_scales, 1)
        nc.sync.dma_start(list_t[:], offs2)
        nc.sync.dma_start(out=wa_raw[:], in_=wa_words[0].rearrange("p n t -> p (n t)").bitcast(I32))
        nc.sync.dma_start(out=table[2][:], in_=tb_runs[2])
        load_scales(nc.sync, wa_plane_raw, wa_scales, 1)
        nc.sync.dma_start(out=table[3][:], in_=tb_runs[3])
        with nc.allow_non_contiguous_dma(reason="one target a partition"):
            nc.sync.dma_start(out=target[:], in_=tg.rearrange("(h p) o -> p (h o)", p=P))
            nc.sync.dma_start(out=weight_pairs[:], in_=cw1.rearrange("o (c p) -> p (o c)", p=P))

        def pick_tokens(name, offsets):
            words = sb.tile([P, J], U16, name=name + "_words", align_bytes=64)
            plane = sb.tile([P, J], U8, name=name + "_plane", align_bytes=64)
            nc.vector.tensor_copy(words[:], x_words[:].indirect(offsets[:]))
            nc.vector.tensor_copy(plane[:], x_plane[:].indirect(offsets[:]))
            return words, plane

        def deal(name, raw, plane_raw, word_copy, view):
            words = sb.tile([P, R], I32, name=name + "_dealt", align_bytes=64)
            plane = sb.tile([P, R], U8, name=name + "_plane_dealt", align_bytes=64)
            word_copy(
                out=words[:].bitcast(view).rearrange("p (t b q) -> p t b q", t=PACK, q=RUN),
                in_=raw[:].bitcast(view).rearrange("p (b t q) -> p t b q", t=PACK, q=RUN),
            )
            nc.scalar.copy(
                out=plane[:].bitcast(U32).rearrange("p (t b q) -> p t b q", t=PACK, q=RUN // 4),
                in_=plane_raw[:].bitcast(U32).rearrange("p (b t q) -> p t b q", t=PACK, q=RUN // 4),
            )
            return words, plane

        def first_stage(target_cols, t, w, w_dtype, x, cols):
            feats = slice(t * P, (t + 1) * P)
            nc.tensor.matmul_mx(
                out=target_cols,
                lhsT=w[0][:, feats].bitcast(w_dtype),
                lhsT_scale=w[1][:, feats],
                rhs=x[0][:, cols].bitcast(E2M1),
                rhs_scale=x[1][:, cols],
                start=True,
                stop=True,
            )

        xb = pick_tokens("xb", list_b)
        wb = deal("wb", wb_raw, wb_plane_raw, nc.scalar.copy, U32)
        xa = pick_tokens("xa", list_a)
        zb = [ps.tile([P, PACK, HALF], F32, name="zb%d" % h, tag="bank%d" % h) for h in range(2)]
        for h in range(2):
            for t in range(PACK):
                first_stage(zb[h][:, t, :], t, wb, E4M3, xb, slice(h * HALF, (h + 1) * HALF))
        wa = deal("wa", wa_raw, wa_plane_raw, nc.vector.tensor_copy, I32)
        za = [ps.tile([P, PACK, HALF], F32, name="za%d" % h) for h in range(2)]
        for h in range(2):
            for t in range(PACK):
                first_stage(za[h][:, t, :], t, wa, E5M2, xa, slice(h * HALF, (h + 1) * HALF))

        picked = sb.tile([P, PACK, J], F32, name="picked", tag="picked", align_bytes=64)
        for t in range(PACK):
            nc.scalar.activation(picked[:, t, :], table[t][:].indirect(list_t[:]), ACT.Copy)

        nb = HALF // BUNDLE
        sums = sb.tile([P, 2, nb, PACK], F32, name="sums", tag="sums")
        means = [sb.tile([P, nb, PACK], F32, name="means%d" % c, tag="means%d" % c) for c in range(2)]
        for c in range(2):
            nc.vector.tensor_reduce(
                out=sums[:, c],
                in_=zb[c][:].rearrange("p t (g e) -> p g t e", e=BUNDLE),
                axis=mybir.AxisListType.X,
                op=ALU.add,
            )
            nc.gpsimd.tensor_scalar(
                means[c][:].rearrange("p g t -> p (g t)"),
                sums[:, c].rearrange("p g t -> p (g t)"),
                1.0 / BUNDLE,
                0.0,
                ALU.mult,
                ALU.add,
            )

        def level(c, tag):
            hb = sb.tile([P, HALF, PACK], BF16, name="hb%d" % c, tag=tag, align_bytes=64)
            nc.vector.tensor_tensor(
                hb[:].rearrange("p (g e) t -> p g e t", e=BUNDLE),
                zb[c][:].rearrange("p t (g e) -> p g e t", e=BUNDLE),
                means[c][:].unsqueeze(2).broadcast_to([P, nb, BUNDLE, PACK]),
                ALU.subtract,
            )
            return hb

        def quantise(name, values):
            words = sb.tile([P, HALF], U32, name=name + "_q", align_bytes=64)
            plane = sb.tile([P, HALF], U8, name=name + "_s", align_bytes=64)
            nc.vector.quantize_mx(
                out=words[:].bitcast(E5M2), scales=plane[:], in_=values[:].rearrange("p c t -> p (c t)")
            )
            return words, plane

        hb = [level(0, "hb0")]
        minus_target = sb.tile([P, 2], F32, name="minus_target", tag="means0")
        nc.gpsimd.tensor_scalar(minus_target[:], target[:], -1.0, 0.0, ALU.mult, ALU.add)
        weight = ps.tile([P, 2, P], F32, name="weight", tag="bank0")
        for e in range(2):
            nc.tensor.transpose(weight[:, e, :], weight_pairs[:, e : e + 1].to_broadcast([P, P]), identity[:])
        diff = sb.tile([P, 2, PACK, HALF], F32, name="diff", tag="sums")
        ha = [sb.tile([P, HALF, PACK], BF16, name="ha%d" % h, align_bytes=64) for h in range(2)]
        for h in range(2):
            nc.vector.tensor_tensor(diff[:, h], za[h][:], picked[:, :, h * HALF : (h + 1) * HALF], ALU.subtract)
            nc.scalar.activation(
                ha[h][:].rearrange("p (c n) t -> p c t n", n=4),
                diff[:, h].rearrange("p t (c n) -> p c t n", n=4),
                ACT.Relu,
            )
        hb.append(level(1, "picked"))
        hbq = [quantise("hb0", hb[0])]
        haq = [quantise("ha0", ha[0])]
        hbq.append(quantise("hb1", hb[1]))
        haq.append(quantise("ha1", ha[1]))

        for h in range(2):
            excess = sb.tile([P, I], F32, name="excess%d" % h)
            for c in range(2):
                score = ps.tile([P, HALF], F32, name="score%d%d" % (h, c))
                nc.tensor.matmul_mx(
                    out=score[:],
                    lhsT=haq[h][0][:].bitcast(E5M2),
                    lhsT_scale=haq[h][1][:],
                    rhs=hbq[c][0][:].bitcast(E5M2),
                    rhs_scale=hbq[c][1][:],
                    start=True,
                    stop=True,
                )
                nc.scalar.activation(
                    excess[:, c * HALF : (c + 1) * HALF], score[:], ACT.Relu, bias=minus_target[:, h : h + 1]
                )
            result = sb.tile([P, I], F32, name="result%d" % h)
            nc.vector.scalar_tensor_tensor(
                result[:], excess[:], 0.04, weight[:].rearrange("p c n -> p (c n)"), ALU.mult, ALU.mult
            )
            nc.sync.dma_start(out=out[h * P : (h + 1) * P, :], in_=result[:])
